import numpy as np
import ml_dtypes


def mxq(x, axis, fmt="e4m3"):
    dtype, down = {"e4m3": (ml_dtypes.float8_e4m3fn, 7), "e5m2": (ml_dtypes.float8_e5m2, 14)}[fmt]
    v = np.moveaxis(np.asarray(x, np.float32).astype(ml_dtypes.bfloat16).astype(np.float64), axis, -1)
    blocks = v.reshape(v.shape[:-1] + (-1, 32))
    amax = np.abs(blocks).max(-1, keepdims=True)
    byte = np.maximum(np.where(amax > 0, np.frexp(amax)[1] - 1 + 127, 0) - down, 1)
    scale = np.exp2(byte - 127.0)
    codes = (blocks / scale).astype(np.float32).astype(dtype).astype(np.float64)
    return np.moveaxis((codes * scale).reshape(v.shape), -1, axis)


WIDE = False


def mx_kscale(k):
    if not WIDE:
        return np.ones(k)
    levels = np.array([10, -10, 5, -5, 0])
    if k % 512:
        return np.exp2(np.random.permutation(np.resize(levels, k // 32))).repeat(32)
    a = np.empty((k // 512, 16))
    for p in range(k // 512):
        a[p, :8] = np.random.permutation(np.resize(levels, 8))
        for g in range(8):
            far = levels[np.abs(levels - a[p, g]) >= 10]
            a[p, g + 8] = far[np.random.randint(len(far))]
    return np.exp2(a.ravel()).repeat(32)


BF16 = ml_dtypes.bfloat16


def bf(x):
    return np.asarray(x, np.float32).astype(BF16)


def f64(x):
    return np.asarray(x).astype(np.float64)


E2M1 = np.array([0.0, 0.5, 1.0, 1.5, 2.0, 3.0, 4.0, 6.0, -0.0, -0.5, -1.0, -1.5, -2.0, -3.0, -4.0, -6.0])


def pack_weight(w, fmt):
    k, n = w.shape
    w = f64(bf(w)).reshape(k // 32, 32, n)
    amax = np.abs(w).max(1)
    if fmt == "e4m3":
        byte = np.frexp(amax)[1] - 1 + 127 - 7
    else:
        mant, ex = np.frexp(amax / 6.0)
        byte = np.where(mant > 0.5, ex, ex - 1) + 127
    byte = np.clip(np.where(amax > 0, byte, 1), 1, 254)
    scaled = (w * np.exp2(127.0 - byte)[:, None, :]).reshape(k, n).astype(np.float32)
    by_word = np.ascontiguousarray(scaled.reshape(k // 512, 128, 4, n).transpose(0, 1, 3, 2))
    if fmt == "e4m3":
        words = by_word.astype(ml_dtypes.float8_e4m3fn).view(np.uint8)
    else:
        c = by_word.astype(ml_dtypes.float4_e2m1fn).view(np.uint8) & 0xF
        words = c[..., 0::2] | (c[..., 1::2] << 4)
    return np.ascontiguousarray(words), np.ascontiguousarray(byte.astype(np.uint8).reshape(k // 512, 16, n))


def unpack_weight(words, scales, fmt):
    g, p, n, _ = words.shape
    if fmt == "e4m3":
        vals = np.ascontiguousarray(words).view(ml_dtypes.float8_e4m3fn).astype(np.float64)
    else:
        nib = np.empty((g, p, n, 4), np.uint8)
        nib[..., 0::2] = words & 0xF
        nib[..., 1::2] = words >> 4
        vals = E2M1[nib]
    vals = vals * np.repeat(np.exp2(scales.astype(np.float64) - 127.0), 8, axis=1)[..., None]
    return vals.transpose(0, 1, 3, 2).reshape(g * 512, n)

def planes(Y):
    n, m = Y.shape
    b = f64(bf(Y)).reshape(n // 32, 32, m)
    amax = np.abs(b).max(1)
    byte = np.clip(np.where(amax > 0, np.frexp(amax)[1] - 1 + 127 - 7, 1), 1, 254)
    codes = (b * np.exp2(127.0 - byte)[:, None, :]).reshape(n, m).astype(np.float32).astype(ml_dtypes.float8_e4m3fn).view(np.uint8)
    words = codes.reshape(n // 512, 128, 4, m).transpose(0, 1, 3, 2)
    return np.ascontiguousarray(words), np.ascontiguousarray(byte.astype(np.uint8).reshape(n // 512, 16, m))


N, D = 2048, 1024


def setup_inputs():
    s, t = mx_kscale(D), mx_kscale(N)
    x = np.random.standard_normal((N, D)) * s
    w = np.random.standard_normal((D, D)) / np.sqrt(D) / s[None, :]
    k = np.random.uniform(-1.0, 1.0, D)
    g = (1.0 + 0.1 * np.random.standard_normal(N)) * t
    h = (1.0 + 0.1 * np.random.standard_normal(N)) / t
    words, scales = pack_weight(w.T, "e4m3")
    return {"x": bf(x), "w_words": words, "w_scales": scales, "k": bf(k), "g": bf(g), "h": bf(h)}


def core(x, w_words, w_scales, k, g, h):
    n = x.shape[0]
    root_n = np.sqrt(n)
    y = mxq(f64(x), 1, "e4m3") @ unpack_weight(w_words, w_scales, "e4m3")
    p = f64(g)[:, None] * (f64(k)[None, :] * np.tanh(y) + y)
    z = f64(h)[:, None] * y
    c = (mxq(p, 0, "e4m3").T @ mxq(z, 0, "e4m3")) / root_n
    return root_n * np.eye(w_words.shape[2]) - c


def reference(x, w_words, w_scales, k, g, h):
    R_out = core(x, w_words, w_scales, k, g, h)
    words, scales = planes(R_out.T)
    return R_out, words, scales

@@ -1,0 +1,440 @@
+import math
+from contextlib import ExitStack
+
+import concourse.mybir as mybir
+from concourse.masks import make_identity
+
+N, D = 2048, 1024
+FLOPS = 2 * N * D * D * 2
+
+F32 = mybir.dt.float32
+BF16 = mybir.dt.bfloat16
+U32 = mybir.dt.uint32
+I32 = mybir.dt.int32
+U8 = mybir.dt.uint8
+FP8X4 = mybir.dt.float8_e4m3fn_x4
+ALU = mybir.AluOpType
+ACT = mybir.ActivationFunctionType
+
+P = 128
+BLK = 256
+ROOT_N = math.sqrt(N)
+
+UNITS = [(0, 0), (1, 0), (2, 0), (0, 1), (1, 1), (0, 2), (1, 2), (0, 3), (1, 3),
+         (2, 1), (2, 2), (2, 3), (3, 0), (3, 1), (3, 2), (3, 3)]
+STEPS = [(0, 0), (1, 0), (0, 1), (1, 1)] + [(u, e) for u in range(2, 16) for e in range(2)]
+POOL_SHARE = [272] + [352] * 14
+NB = 2
+POOL_COLS = 352
+REST_ENG = "vvvvvaaaaaaavvvv"
+NY = 3
+X_TURN = {1: [5, 6], 2: [7], 3: [8], 4: [9], 5: [10], 6: [11], 7: [12], 8: [13], 9: [14], 10: [15]}
+X_COPY = "avavaaaaaaaaaaaa"
+X_BANK = [4, 5, 6, 7, 4, 5, 6, 7, 4, 5, 4, 5, 4, 5, 4, 5]
+JOBS = [(0, 0, 512, 6, 8, "a"), (1, 0, 512, 7, 8, "a"), (2, 0, 512, 4, 13, "a"), (3, 0, 512, 5, 14, "a"),
+        (0, 512, 256, 4, 25, "a"), (1, 512, 256, 5, 26, "a"), (4, 0, 512, 6, 22, "a"), (5, 0, 512, 7, 23, "a"),
+        (2, 512, 256, 4, 28, "a"), (3, 512, 256, 5, 28, "a"), (4, 512, 256, 6, 29, "a"), (5, 512, 256, 7, 29, "a"),
+        (6, 0, 512, 5, 30, "a"), (7, 0, 512, 6, 31, "v"), (6, 512, 512, 7, 31, "a"), (7, 512, 512, 4, 32, "v"),
+        (0, 768, 256, 3, 31, "a"), (1, 768, 256, 1, 32, "v"), (2, 768, 256, 2, 32, "a"), (3, 768, 256, 0, 32, "v")]
+TURNS = {23: (0, 0, 4), 24: (1, 0, 5), 30: (2, 0, 4)}
+EMPTY_MAX = 2
+CAST_ENG = "v"
+TAIL_ACT_COLS = 192
+TAIL_P_COLS = 64
+TAIL_CAST = "vvvvvvvvvv"
+
+
+def p_at(col):
+    b = col // BLK
+    return 512 * b + (BLK if b % 2 else 0) + col % BLK
+
+
+def z_at(col):
+    b = col // BLK
+    return 512 * b + (0 if b % 2 else BLK) + col % BLK
+
+
+def tile_extendedinfomaxnaturalgradient_x2_kernel(tc, x, w_words, w_scales, k, g, h, out_0, out_1, out_2):
+    nc = tc.nc
+    with ExitStack() as ctx:
+        sb = ctx.enter_context(tc.tile_pool(name="sb", bufs=1))
+        ps = ctx.enter_context(tc.psum_pool(name="ps", bufs=1))
+        ctx.enter_context(tc.manual_schedule())
+
+        banks = [ps.tile([P, 512], F32, name="bank%d" % b) for b in range(8)]
+        x_raw = [sb.tile([P, D], BF16, name="x_raw%d" % m, align_bytes=64) for m in range(16)]
+        x_il = sb.tile([P, 8, D], BF16, name="x_il", align_bytes=64)
+        x_codes = sb.tile([P, 16 * 256], U32, name="x_codes", align_bytes=64)
+        x_scales = sb.tile([P, 16 * 256], U8, name="x_scales", align_bytes=64)
+        w_codes = [sb.tile([P, 2, BLK], U32, name="w_codes%d" % a, align_bytes=64) for a in range(4)]
+        w_plane = sb.tile([P, D], U8, name="w_plane", align_bytes=64)
+        k_cols = sb.tile([P, 2, 4], BF16, name="k_cols")
+        g_raw = sb.tile([P, 4, 4], BF16, name="g_raw")
+        h_raw = sb.tile([P, 4, 4], BF16, name="h_raw")
+        g_col = sb.tile([P, 4, 4], F32, name="g_col")
+        h_col = sb.tile([P, 4, 4], F32, name="h_col")
+        ident = sb.tile([P, P], F32, name="ident")
+        ident_bf = sb.tile([P, P], BF16, name="ident_bf")
+        ident_root = sb.tile([P, P], F32, name="ident_root")
+        warm = sb.tile([P, 2], F32, name="warm")
+        tanh_y = [sb.tile([P, 512], F32, name="tanh_y%d" % a) for a in range(3)]
+        gk_tanh = [sb.tile([P, BLK], F32, name="gk_tanh%d" % a) for a in range(2)]
+        stage = [sb.tile([P, 4, 512], BF16, name="stage%d" % a, align_bytes=64) for a in range(3)]
+        chunk_cols = BLK * NB
+        pool_cols = POOL_COLS * NB // 2
+        rest_cols = chunk_cols - pool_cols
+        il = sb.tile([P, 2 * rest_cols + pool_cols, 4], BF16, name="il", align_bytes=64)
+        il_tail = sb.tile([P, 512, 4], BF16, name="il_tail", align_bytes=64)
+        pz_codes = sb.tile([P, 4, 2048], U32, name="pz_codes", align_bytes=64)
+        pz_scales = sb.tile([P, 4, 2048], U8, name="pz_scales", align_bytes=64)
+        r32 = sb.tile([P, 8, D], F32, name="r32")
+        r16 = sb.tile([P, 8, 2, 2, P, 2], BF16, name="r16", align_bytes=64)
+        r_il = [sb.tile([P, 2, P, 4], BF16, name="r_il%d" % a, align_bytes=64) for a in range(3)]
+        o_codes = sb.tile([P, 2, D], U32, name="o_codes", align_bytes=64)
+        o_scales = sb.tile([P, 2, D], U8, name="o_scales", align_bytes=64)
+
+        k_bank = banks[0][:].bitcast(BF16)
+        y_banks = banks[1:1 + NY]
+
+        x_rows = x.rearrange("(a p t) j -> a t p j", p=P, t=4)
+        w_view = w_words.rearrange("a p n t -> p a (n t)")
+
+        def load_x(m):
+            nc.sync.dma_start(out=x_raw[m][:], in_=x_rows[m // 4, m % 4])
+
+        def load_w(half):
+            nc.sync.dma_start(out=w_codes[half][:].bitcast(I32), in_=w_view[:, :, 1024 * half:1024 * (half + 1)].bitcast(I32))
+
+        make_identity(nc, ident[:])
+        nc.vector.memset(w_plane[:].bitcast(I32), 0)
+        nc.vector.memset(warm[:], 0.0)
+        nc.scalar.dma_start(out=k_cols[:], in_=k.rearrange("(a p c) -> p a c", a=2, c=4))
+        load_x(0)
+        load_x(1)
+        load_w(0)
+        for q in range(4):
+            nc.scalar.dma_start(out=w_plane[32 * q:32 * q + 8, :].bitcast(I32), in_=w_scales[:, 4 * q:4 * q + 4, :].bitcast(I32))
+        nc.scalar.activation(out=warm[:, 1:2], in_=warm[:, 0:1], func=ACT.Tanh)
+        nc.gpsimd.dma_start(out=h_raw[:], in_=h.rearrange("(a p t) -> p a t", a=4, t=4))
+        nc.gpsimd.dma_start(out=g_raw[:], in_=g.rearrange("(a p t) -> p a t", a=4, t=4))
+        for m in range(2, 16):
+            load_x(m)
+            if m == 2:
+                load_w(1)
+            if m == 5:
+                load_w(2)
+        load_w(3)
+        nc.vector.tensor_copy(out=ident_bf[:], in_=ident[:])
+        nc.vector.tensor_scalar(out=ident_root[:], in0=ident[:], scalar1=ROOT_N, scalar2=None, op0=ALU.mult)
+
+        def turn_x(m):
+            words = x_raw[m][:].bitcast(F32)
+            bank = banks[X_BANK[m]]
+            for a in range(2):
+                for u in range(2):
+                    c = (2 * a + u) * P
+                    nc.tensor.transpose(bank[:, c:c + P], words[:, 256 * a + u:256 * (a + 1):2], ident[:])
+
+        def copy_x(m, eng):
+            src = banks[X_BANK[m]][:].rearrange("p (a u r) -> p a r u", a=2, u=2)
+            dst = x_il[:, m % 8, :].bitcast(F32).rearrange("p (a r u) -> p a r u", a=2, u=2)
+            if eng == "a":
+                nc.scalar.copy(out=dst, in_=src)
+            else:
+                nc.vector.tensor_copy(out=dst, in_=src)
+
+        def quantize_x(m, count):
+            cols = slice(256 * m, 256 * (m + count))
+            nc.vector.quantize_mx(out=x_codes[:, cols].bitcast(FP8X4), scales=x_scales[:, cols],
+                                  in_=x_il[:, m % 8:m % 8 + count, :].rearrange("p a c -> p (a c)"))
+
+        def spread_k(a):
+            for c in range(4):
+                    o = (4 * a + c) * P
+                    nc.tensor.transpose(k_bank[:, o:o + P], k_cols[:, a, c:c + 1].to_broadcast([P, P]), ident_bf[:])
+
+        def y_step(s, tiles=(0, 1)):
+            unit, half = STEPS[s]
+            b, grp = UNITS[unit]
+            bank = y_banks[s % NY]
+            for e in tiles:
+                m = 4 * grp + 2 * half + e
+                for a in range(2):
+                    xc = slice(256 * m + P * a, 256 * m + P * (a + 1))
+                    nc.tensor.matmul_mx(out=bank[:, BLK * e:BLK * (e + 1)], lhsT=x_codes[:, xc].bitcast(FP8X4), lhsT_scale=x_scales[:, xc],
+                                        rhs=w_codes[b][:, a, :].bitcast(FP8X4), rhs_scale=w_plane[4 * a:, BLK * b:BLK * (b + 1)],
+                                        start=(a == 0), stop=(a == 1))
+
+        def scalar_step(s):
+            unit, half = STEPS[s]
+            b, grp = UNITS[unit]
+            bank = y_banks[s % NY]
+            nc.scalar.activation(out=tanh_y[s % 3][:], in_=bank[:], func=ACT.Tanh)
+            zc = z_at(BLK * b) - 512 * b
+            for e in range(2):
+                t = 2 * half + e
+                nc.scalar.activation(out=stage[unit % 3][:, t, zc:zc + BLK], in_=bank[:, BLK * e:BLK * (e + 1)],
+                                     func=ACT.Copy, scale=h_col[:, grp, t:t + 1])
+
+        def vector_step(s):
+            unit, half = STEPS[s]
+            b, grp = UNITS[unit]
+            bank = y_banks[s % NY]
+            pc = p_at(BLK * b) - 512 * b
+            k_row = k_bank[:, 512 * (b // 2):512 * (b // 2 + 1)].rearrange("p (c r) -> p r c", c=4)[:, 64 * (b % 2):64 * (b % 2 + 1), :]
+            for e in range(2):
+                t = 2 * half + e
+                nc.vector.scalar_tensor_tensor(out=gk_tanh[e][:].rearrange("p (r c) -> p r c", c=4),
+                                               in0=tanh_y[s % 3][:, BLK * e:BLK * (e + 1)].rearrange("p (r c) -> p r c", c=4),
+                                               scalar=g_col[:, grp, t:t + 1], in1=k_row, op0=ALU.mult, op1=ALU.mult)
+            for e in range(2):
+                t = 2 * half + e
+                nc.vector.scalar_tensor_tensor(out=stage[unit % 3][:, t, pc:pc + BLK], in0=bank[:, BLK * e:BLK * (e + 1)],
+                                               scalar=g_col[:, grp, t:t + 1], in1=gk_tanh[e][:], op0=ALU.mult, op1=ALU.add)
+
+        def interleave(eng, dst, unit, c0, cols):
+            src = stage[unit % 3][:, :, c0:c0 + cols].rearrange("p t c -> p c t")
+            if eng == "p":
+                nc.gpsimd.tensor_scalar(out=dst, in0=src, scalar1=1.0, scalar2=1.0, op0=ALU.mult, op1=ALU.mult)
+            elif eng == "a":
+                nc.scalar.copy(out=dst, in_=src)
+            else:
+                nc.vector.tensor_copy(out=dst, in_=src)
+
+        def chunk_base(c):
+            return 0 if c % 2 == 0 else rest_cols
+
+        def chunk_pool(c):
+            n = POOL_SHARE[c]
+            c0 = 512 - n if c % 2 == 0 else 0
+            interleave("p", il[:, chunk_base(c) + c0:chunk_base(c) + c0 + n, :], c, c0, n)
+
+        def chunk_rest(c, eng):
+            n = 512 - POOL_SHARE[c]
+            c0 = 0 if c % 2 == 0 else 512 - n
+            interleave(eng, il[:, chunk_base(c) + c0:chunk_base(c) + c0 + n, :], c, c0, n)
+
+        made = {}
+
+        def quantize_pz(unit, c0, cols, src, it):
+            b, grp = UNITS[unit]
+            at = slice(512 * b + c0, 512 * b + c0 + cols)
+            nc.vector.quantize_mx(out=pz_codes[:, grp, at].bitcast(FP8X4), scales=pz_scales[:, grp, at], in_=src.rearrange("p c t -> p (c t)"))
+            for c in range(512 * b + c0, 512 * b + c0 + cols, BLK):
+                made[(grp, c // BLK)] = it
+
+        def chunk_quantize(c, it):
+            quantize_pz(c, 0, 512, il[:, chunk_base(c):chunk_base(c) + 512, :], it)
+
+        passes_done = {}
+        to_empty = []
+        to_cast = []
+        to_copy = []
+        to_quant = []
+        stored = []
+
+        def ready(job, grp, it):
+            i, j0, w = job[:3]
+            need = [p_at(P * i) // BLK] + [z_at(c) // BLK for c in range(j0, j0 + w, BLK)]
+            return all((grp, c) in made and made[(grp, c)] < it for c in need)
+
+        def r_pass(job, grp):
+            i, j0, w, b = job[:4]
+            pc = slice(p_at(P * i), p_at(P * i) + P)
+            zc = slice(z_at(j0), z_at(j0) + w)
+            nc.tensor.matmul_mx(out=banks[b][:, 0:w], lhsT=pz_codes[:, grp, pc].bitcast(FP8X4), lhsT_scale=pz_scales[:, grp, pc],
+                                rhs=pz_codes[:, grp, zc].bitcast(FP8X4), rhs_scale=pz_scales[:, grp, zc], start=(grp == 0), stop=(grp == 3))
+
+        def r_passes(it):
+            for job in JOBS:
+                while job[4] <= it and passes_done.get(job, 0) < 4 and ready(job, passes_done.get(job, 0), it):
+                    r_pass(job, passes_done.get(job, 0))
+                    passes_done[job] = passes_done.get(job, 0) + 1
+                    if passes_done[job] == 4:
+                        to_empty.append((job, it))
+
+        def empty_job(job, it):
+            i, j0, w, b, first, eng = job
+            if eng == "a":
+                nc.scalar.activation(out=r32[:, i, j0:j0 + w], in_=banks[b][:, 0:w], func=ACT.Copy, scale=-1.0 / ROOT_N)
+            else:
+                nc.vector.tensor_scalar(out=r32[:, i, j0:j0 + w], in0=banks[b][:, 0:w], scalar1=-1.0 / ROOT_N, scalar2=None, op0=ALU.mult)
+            to_cast.append((job, it))
+
+        def fix_job(job):
+            i, j0, w, b = job[:4]
+            d = P * i - j0
+            if 0 <= d < w:
+                nc.vector.scalar_tensor_tensor(out=r32[:, i, P * i:P * (i + 1)], in0=banks[b][:, d:d + P], scalar=-1.0 / ROOT_N,
+                                               in1=ident_root[:], op0=ALU.mult, op1=ALU.add)
+            nc.sync.dma_start(out=out_0[P * i:P * (i + 1), j0:j0 + w], in_=r32[:, i, j0:j0 + w])
+
+        def cast_job(job, eng):
+            i, j0, w = job[:3]
+            a, r0 = j0 // 512, (j0 % 512) // 4
+            dst = r16[:, i, a, :, r0:r0 + w // 4, :]
+            src = r32[:, i, j0:j0 + w].rearrange("p (r u e) -> p u r e", u=2, e=2)
+            if eng == "p":
+                nc.gpsimd.tensor_scalar(out=dst, in0=src, scalar1=1.0, scalar2=1.0, op0=ALU.mult, op1=ALU.mult)
+            elif eng == "a":
+                nc.scalar.copy(out=dst, in_=src)
+            else:
+                nc.vector.tensor_copy(out=dst, in_=src)
+
+        def turn_pair(pair, a, b, it):
+            for e in range(2):
+                for u in range(2):
+                    c = (2 * e + u) * P
+                    nc.tensor.transpose(banks[b][:, c:c + P], r16[:, 2 * pair + e, a, u].rearrange("p r e -> p (r e)").bitcast(F32), ident[:])
+            to_copy.append((pair, a, b, it))
+
+        def copy_pair(it, eng):
+            pair, a, b, was = to_copy.pop(0)
+            slot = len(stored) % 3
+            stored.append(pair)
+            src = banks[b][:].rearrange("p (e u r) -> p e r u", e=2, u=2)
+            dst = r_il[slot][:].rearrange("p e r t -> p (e r t)").bitcast(F32).rearrange("p (e r u) -> p e r u", e=2, u=2)
+            if eng == "a":
+                nc.scalar.copy(out=dst, in_=src)
+            else:
+                nc.vector.tensor_copy(out=dst, in_=src)
+            to_quant.append((pair, a, slot, it))
+
+        def quantize_pair():
+            pair, a, slot, was = to_quant.pop(0)
+            at = slice(BLK * pair, BLK * (pair + 1))
+            nc.vector.quantize_mx(out=o_codes[:, a, at].bitcast(FP8X4), scales=o_scales[:, a, at], in_=r_il[slot][:].rearrange("p e r t -> p (e r t)"))
+            nc.sync.dma_start(out=out_1[a].rearrange("p m t -> p (m t)")[:, 4 * BLK * pair:4 * BLK * (pair + 1)].bitcast(I32), in_=o_codes[:, a, at].bitcast(I32))
+
+        n_steps = len(STEPS)
+        spread_k(0)
+        turn_x(0)
+        turn_x(1)
+        copy_x(0, X_COPY[0])
+        quantize_x(0, 1)
+        copy_x(1, X_COPY[1])
+        nc.vector.tensor_copy(out=h_col[:], in_=h_raw[:])
+        quantize_x(1, 1)
+        nc.vector.tensor_copy(out=g_col[:], in_=g_raw[:])
+        turn_x(2)
+        y_step(0)
+        y_step(1)
+        turn_x(3)
+        copy_x(2, X_COPY[2])
+        scalar_step(0)
+        quantize_x(2, 1)
+        copy_x(3, X_COPY[3])
+        vector_step(0)
+        quantize_x(3, 1)
+        turn_x(4)
+        y_step(2)
+        scalar_step(1)
+        spread_k(1)
+        x_done = 4
+        x_copied = 4
+        x_turned = 5
+        chunk = 0
+        pending = None
+        for s in range(1, n_steps):
+            x_to_copy = x_turned
+            if s + 2 < n_steps:
+                y_step(s + 2)
+            for m in X_TURN.get(s, []):
+                turn_x(m)
+                x_turned += 1
+            if s in TURNS:
+                turn_pair(*TURNS[s], s)
+            r_passes(s)
+            fresh = pending is None and (chunk, 1) in STEPS[:max(s, 0)] and chunk <= s // 2 - 1
+            if fresh:
+                pending = chunk
+                chunk += 1
+                chunk_pool(pending)
+            while x_copied < x_to_copy:
+                copy_x(x_copied, X_COPY[x_copied])
+                x_copied += 1
+            if to_copy and to_copy[0][3] < s:
+                copy_pair(s, "a")
+            fixes = []
+            while to_empty and to_empty[0][1] < s and len(fixes) < EMPTY_MAX:
+                job, was = to_empty.pop(0)
+                empty_job(job, s)
+                fixes.append(job)
+            if 0 < s + 1 < n_steps:
+                scalar_step(s + 1)
+            if fresh and REST_ENG[pending] == "a":
+                chunk_rest(pending, "a")
+            if s >= 0:
+                vector_step(s)
+            for job in fixes:
+                fix_job(job)
+            if s % NB == NB - 1:
+                if pending is not None and REST_ENG[pending] == "v":
+                    chunk_rest(pending, "v")
+                while x_done < x_copied:
+                    count = 2 if (x_copied - x_done >= 2 and x_done % 2 == 0) else 1
+                    quantize_x(x_done, count)
+                    x_done += count
+                while to_cast:
+                    job, was = to_cast.pop(0)
+                    cast_job(job, CAST_ENG)
+                while to_quant:
+                    quantize_pair()
+                if pending is not None:
+                    chunk_quantize(pending, s)
+                    pending = None
+        last = len(UNITS) - 1
+        it = n_steps
+        interleave("a", il_tail[:, 0:TAIL_ACT_COLS, :], last, 0, TAIL_ACT_COLS)
+        interleave("v", il_tail[:, TAIL_ACT_COLS:BLK, :], last, TAIL_ACT_COLS, BLK - TAIL_ACT_COLS)
+        r_passes(it)
+        interleave("a", il_tail[:, BLK:BLK + TAIL_P_COLS, :], last, BLK, TAIL_P_COLS)
+        interleave("v", il_tail[:, BLK + TAIL_P_COLS:512, :], last, BLK + TAIL_P_COLS, BLK - TAIL_P_COLS)
+        quantize_pz(last, 0, BLK, il_tail[:, 0:BLK, :], it)
+        quantize_pz(last, BLK, BLK, il_tail[:, BLK:512, :], it)
+        wide = JOBS[12:16]
+        narrow = JOBS[16:20]
+        late = [(4, 768, 256, narrow[0][3], it, "a"), (5, 768, 256, narrow[1][3], it, "v")]
+        for job in narrow + wide:
+            r_pass(job, 3)
+
+        def finish(a, b):
+            for job in (a, b):
+                empty_job(job, it)
+                fix_job(job)
+
+        def casts(a, b):
+            for job in (a, b):
+                cast_job(job, TAIL_CAST[len(stored)])
+
+        finish(*narrow[0:2])
+        for job in late:
+            for grp in range(4):
+                r_pass(job, grp)
+        finish(*narrow[2:4])
+        casts(*narrow[0:2])
+        finish(*wide[0:2])
+        casts(*narrow[2:4])
+        turn_pair(0, 1, narrow[2][3], it)
+        turn_pair(1, 1, narrow[3][3], it)
+        finish(*wide[2:4])
+        casts(*wide[0:2])
+        copy_pair(it, "a")
+        turn_pair(3, 0, wide[0][3], it)
+        finish(*late)
+        casts(*wide[2:4])
+        quantize_pair()
+        copy_pair(it, "a")
+        turn_pair(3, 1, wide[1][3], it)
+        casts(*late)
+        turn_pair(2, 1, wide[2][3], it)
+        copy_pair(it, "a")
+        quantize_pair()
+        quantize_pair()
+        copy_pair(it, "v")
+        copy_pair(it, "a")
+        quantize_pair()
+        quantize_pair()
+        for q in range(4):
+            eng = nc.sync if q % 2 else nc.scalar
+            eng.dma_start(out=out_2[:, 4 * q:4 * q + 4, :].rearrange("a r m -> r a m").bitcast(I32), in_=o_scales[32 * q:32 * q + 4, :, :].bitcast(I32))

@@ -26,22 +26,21 @@ STEPS = [(0, 0), (1, 0), (0, 1), (1, 1)] + [(u, e) for u in range(2, 16) for e i
 POOL_SHARE = [272] + [352] * 14
 NB = 2
 POOL_COLS = 352
-REST_ENG = "vvvvvaaaaaaavvvv"
 NY = 3
 X_TURN = {1: [5, 6], 2: [7], 3: [8], 4: [9], 5: [10], 6: [11], 7: [12], 8: [13], 9: [14], 10: [15]}
-X_COPY = "avavaaaaaaaaaaaa"
+X_COPY = "avaaaaaaaaaaaaaa"
 X_BANK = [4, 5, 6, 7, 4, 5, 6, 7, 4, 5, 4, 5, 4, 5, 4, 5]
-JOBS = [(0, 0, 512, 6, 8, "a"), (1, 0, 512, 7, 8, "a"), (2, 0, 512, 4, 13, "a"), (3, 0, 512, 5, 14, "a"),
-        (0, 512, 256, 4, 25, "a"), (1, 512, 256, 5, 26, "a"), (4, 0, 512, 6, 22, "a"), (5, 0, 512, 7, 23, "a"),
-        (2, 512, 256, 4, 28, "a"), (3, 512, 256, 5, 28, "a"), (4, 512, 256, 6, 29, "a"), (5, 512, 256, 7, 29, "a"),
-        (6, 0, 512, 5, 30, "a"), (7, 0, 512, 6, 31, "v"), (6, 512, 512, 7, 31, "a"), (7, 512, 512, 4, 32, "v"),
-        (0, 768, 256, 3, 31, "a"), (1, 768, 256, 1, 32, "v"), (2, 768, 256, 2, 32, "a"), (3, 768, 256, 0, 32, "v")]
-TURNS = {23: (0, 0, 4), 24: (1, 0, 5), 30: (2, 0, 4)}
+JOBS = [((0,), 0, 512, 6, 8, "a"), ((1,), 0, 512, 7, 8, "a"), ((2,), 0, 512, 4, 13, "a"), ((3,), 0, 512, 5, 14, "a"),
+        ((4,), 0, 512, 6, 22, "a"), ((5,), 0, 512, 7, 23, "a"), ((0, 1), 512, 256, 4, 25, "a"), ((2, 3), 512, 256, 5, 27, "a"),
+        ((4, 5), 512, 256, 6, 28, "a"), ((6,), 0, 512, 7, 28, "a"), ((7,), 0, 512, 5, 29, "v"), ((6,), 512, 512, 6, 30, "a"),
+        ((7,), 512, 512, 4, 31, "v"), ((0,), 768, 256, 3, 30, "a"), ((1,), 768, 256, 1, 31, "v"), ((2, 3), 768, 256, 0, 32, "a"),
+        ((4, 5), 768, 256, 2, 32, "v")]
+TURNS = {23: (0, 0, 4), 24: (1, 0, 5), 29: (2, 0, 4)}
 EMPTY_MAX = 2
+ACT_SHARE = [0, 0, 0, 0, 0, 160, 160, 160, 160, 160, 160, 160, 0, 0, 160]
+FAST_IL = True
 CAST_ENG = "v"
-TAIL_ACT_COLS = 192
-TAIL_P_COLS = 64
-TAIL_CAST = "vvvvvvvvvv"
+TAIL_P_COLS = 96
 
 
 def p_at(col):
@@ -89,7 +88,7 @@ def tile_extendedinfomaxnaturalgradient_x2_kernel(tc, x, w_words, w_scales, k, g
         pz_scales = sb.tile([P, 4, 2048], U8, name="pz_scales", align_bytes=64)
         r32 = sb.tile([P, 8, D], F32, name="r32")
         r16 = sb.tile([P, 8, 2, 2, P, 2], BF16, name="r16", align_bytes=64)
-        r_il = [sb.tile([P, 2, P, 4], BF16, name="r_il%d" % a, align_bytes=64) for a in range(3)]
+        r_il = [sb.tile([P, 2, P, 4], BF16, name="r_il%d" % a, align_bytes=64) for a in range(4)]
         o_codes = sb.tile([P, 2, D], U32, name="o_codes", align_bytes=64)
         o_scales = sb.tile([P, 2, D], U8, name="o_scales", align_bytes=64)
 
@@ -196,7 +195,11 @@ def tile_extendedinfomaxnaturalgradient_x2_kernel(tc, x, w_words, w_scales, k, g
             src = stage[unit % 3][:, :, c0:c0 + cols].rearrange("p t c -> p c t")
             if eng == "p":
                 nc.gpsimd.tensor_scalar(out=dst, in0=src, scalar1=1.0, scalar2=1.0, op0=ALU.mult, op1=ALU.mult)
-            elif eng == "a":
+                return
+            if FAST_IL:
+                dst = dst.rearrange("p (c i) t -> p c t i", i=4)
+                src = src.rearrange("p (c i) t -> p c t i", i=4)
+            if eng == "a":
                 nc.scalar.copy(out=dst, in_=src)
             else:
                 nc.vector.tensor_copy(out=dst, in_=src)
@@ -210,9 +213,11 @@ def tile_extendedinfomaxnaturalgradient_x2_kernel(tc, x, w_words, w_scales, k, g
             interleave("p", il[:, chunk_base(c) + c0:chunk_base(c) + c0 + n, :], c, c0, n)
 
         def chunk_rest(c, eng):
-            n = 512 - POOL_SHARE[c]
-            c0 = 0 if c % 2 == 0 else 512 - n
-            interleave(eng, il[:, chunk_base(c) + c0:chunk_base(c) + c0 + n, :], c, c0, n)
+            n = ACT_SHARE[c] if eng == "a" else 512 - POOL_SHARE[c] - ACT_SHARE[c]
+            edge = 0 if eng == "a" else ACT_SHARE[c]
+            c0 = edge if c % 2 == 0 else 512 - edge - n
+            if n:
+                interleave(eng, il[:, chunk_base(c) + c0:chunk_base(c) + c0 + n, :], c, c0, n)
 
         made = {}
 
@@ -233,53 +238,60 @@ def tile_extendedinfomaxnaturalgradient_x2_kernel(tc, x, w_words, w_scales, k, g
         to_quant = []
         stored = []
 
-        def ready(job, grp, it):
-            i, j0, w = job[:3]
-            need = [p_at(P * i) // BLK] + [z_at(c) // BLK for c in range(j0, j0 + w, BLK)]
-            return all((grp, c) in made and made[(grp, c)] < it for c in need)
+        def ready(job, n, it):
+            tiles, j0, w = job[:3]
+            need = [p_at(P * tiles[n // 4]) // BLK] + [z_at(c) // BLK for c in range(j0, j0 + w, BLK)]
+            return all((n % 4, c) in made and made[(n % 4, c)] < it for c in need)
 
-        def r_pass(job, grp):
-            i, j0, w, b = job[:4]
-            pc = slice(p_at(P * i), p_at(P * i) + P)
+        def r_pass(job):
+            tiles, j0, w, b = job[:4]
+            n = passes_done.get(job, 0)
+            passes_done[job] = n + 1
+            e, grp = divmod(n, 4)
+            pc = slice(p_at(P * tiles[e]), p_at(P * tiles[e]) + P)
             zc = slice(z_at(j0), z_at(j0) + w)
-            nc.tensor.matmul_mx(out=banks[b][:, 0:w], lhsT=pz_codes[:, grp, pc].bitcast(FP8X4), lhsT_scale=pz_scales[:, grp, pc],
+            nc.tensor.matmul_mx(out=banks[b][:, w * e:w * (e + 1)], lhsT=pz_codes[:, grp, pc].bitcast(FP8X4), lhsT_scale=pz_scales[:, grp, pc],
                                 rhs=pz_codes[:, grp, zc].bitcast(FP8X4), rhs_scale=pz_scales[:, grp, zc], start=(grp == 0), stop=(grp == 3))
 
         def r_passes(it):
             for job in JOBS:
-                while job[4] <= it and passes_done.get(job, 0) < 4 and ready(job, passes_done.get(job, 0), it):
-                    r_pass(job, passes_done.get(job, 0))
-                    passes_done[job] = passes_done.get(job, 0) + 1
-                    if passes_done[job] == 4:
+                total = 4 * len(job[0])
+                while job[4] <= it and passes_done.get(job, 0) < total and ready(job, passes_done.get(job, 0), it):
+                    r_pass(job)
+                    if passes_done[job] == total:
                         to_empty.append((job, it))
 
-        def empty_job(job, it):
-            i, j0, w, b, first, eng = job
+        def empty_job(job, eng):
+            tiles, j0, w, b = job[:4]
+            dst = r32[:, tiles[0]:tiles[-1] + 1, j0:j0 + w]
+            src = banks[b][:, 0:w * len(tiles)].rearrange("p (e c) -> p e c", c=w)
             if eng == "a":
-                nc.scalar.activation(out=r32[:, i, j0:j0 + w], in_=banks[b][:, 0:w], func=ACT.Copy, scale=-1.0 / ROOT_N)
+                nc.scalar.activation(out=dst, in_=src, func=ACT.Copy, scale=-1.0 / ROOT_N)
             else:
-                nc.vector.tensor_scalar(out=r32[:, i, j0:j0 + w], in0=banks[b][:, 0:w], scalar1=-1.0 / ROOT_N, scalar2=None, op0=ALU.mult)
-            to_cast.append((job, it))
+                nc.vector.tensor_scalar(out=dst, in0=src, scalar1=-1.0 / ROOT_N, scalar2=None, op0=ALU.mult)
 
         def fix_job(job):
-            i, j0, w, b = job[:4]
-            d = P * i - j0
-            if 0 <= d < w:
-                nc.vector.scalar_tensor_tensor(out=r32[:, i, P * i:P * (i + 1)], in0=banks[b][:, d:d + P], scalar=-1.0 / ROOT_N,
-                                               in1=ident_root[:], op0=ALU.mult, op1=ALU.add)
-            nc.sync.dma_start(out=out_0[P * i:P * (i + 1), j0:j0 + w], in_=r32[:, i, j0:j0 + w])
+            tiles, j0, w, b = job[:4]
+            for e, i in enumerate(tiles):
+                d = P * i - j0
+                if 0 <= d < w:
+                    nc.vector.scalar_tensor_tensor(out=r32[:, i, P * i:P * (i + 1)], in0=banks[b][:, w * e + d:w * e + d + P], scalar=-1.0 / ROOT_N,
+                                                   in1=ident_root[:], op0=ALU.mult, op1=ALU.add)
+            rows = out_0[P * tiles[0]:P * (tiles[-1] + 1), j0:j0 + w].rearrange("(e p) c -> p e c", p=P)
+            nc.sync.dma_start(out=rows, in_=r32[:, tiles[0]:tiles[-1] + 1, j0:j0 + w])
 
         def cast_job(job, eng):
-            i, j0, w = job[:3]
+            tiles, j0, w = job[:3]
             a, r0 = j0 // 512, (j0 % 512) // 4
-            dst = r16[:, i, a, :, r0:r0 + w // 4, :]
-            src = r32[:, i, j0:j0 + w].rearrange("p (r u e) -> p u r e", u=2, e=2)
-            if eng == "p":
-                nc.gpsimd.tensor_scalar(out=dst, in0=src, scalar1=1.0, scalar2=1.0, op0=ALU.mult, op1=ALU.mult)
-            elif eng == "a":
-                nc.scalar.copy(out=dst, in_=src)
-            else:
-                nc.vector.tensor_copy(out=dst, in_=src)
+            for i in tiles:
+                dst = r16[:, i, a, :, r0:r0 + w // 4, :]
+                src = r32[:, i, j0:j0 + w].rearrange("p (r u e) -> p u r e", u=2, e=2)
+                if eng == "p":
+                    nc.gpsimd.tensor_scalar(out=dst, in0=src, scalar1=1.0, scalar2=1.0, op0=ALU.mult, op1=ALU.mult)
+                elif eng == "a":
+                    nc.scalar.copy(out=dst, in_=src)
+                else:
+                    nc.vector.tensor_copy(out=dst, in_=src)
 
         def turn_pair(pair, a, b, it):
             for e in range(2):
@@ -290,7 +302,7 @@ def tile_extendedinfomaxnaturalgradient_x2_kernel(tc, x, w_words, w_scales, k, g
 
         def copy_pair(it, eng):
             pair, a, b, was = to_copy.pop(0)
-            slot = len(stored) % 3
+            slot = len(stored) % 4
             stored.append(pair)
             src = banks[b][:].rearrange("p (e u r) -> p e r u", e=2, u=2)
             dst = r_il[slot][:].rearrange("p e r t -> p (e r t)").bitcast(F32).rearrange("p (e r u) -> p e r u", e=2, u=2)
@@ -318,16 +330,16 @@ def tile_extendedinfomaxnaturalgradient_x2_kernel(tc, x, w_words, w_scales, k, g
         nc.vector.tensor_copy(out=g_col[:], in_=g_raw[:])
         turn_x(2)
         y_step(0)
-        y_step(1)
         turn_x(3)
+        y_step(1)
         copy_x(2, X_COPY[2])
         scalar_step(0)
         quantize_x(2, 1)
-        copy_x(3, X_COPY[3])
         vector_step(0)
+        copy_x(3, X_COPY[3])
         quantize_x(3, 1)
-        turn_x(4)
         y_step(2)
+        turn_x(4)
         scalar_step(1)
         spread_k(1)
         x_done = 4
@@ -335,7 +347,7 @@ def tile_extendedinfomaxnaturalgradient_x2_kernel(tc, x, w_words, w_scales, k, g
         x_turned = 5
         chunk = 0
         pending = None
-        for s in range(1, n_steps):
+        for s in range(1, n_steps - 1):
             x_to_copy = x_turned
             if s + 2 < n_steps:
                 y_step(s + 2)
@@ -358,80 +370,83 @@ def tile_extendedinfomaxnaturalgradient_x2_kernel(tc, x, w_words, w_scales, k, g
             fixes = []
             while to_empty and to_empty[0][1] < s and len(fixes) < EMPTY_MAX:
                 job, was = to_empty.pop(0)
-                empty_job(job, s)
+                empty_job(job, job[5])
+                to_cast.append(job)
                 fixes.append(job)
             if 0 < s + 1 < n_steps:
                 scalar_step(s + 1)
-            if fresh and REST_ENG[pending] == "a":
+            if fresh:
                 chunk_rest(pending, "a")
             if s >= 0:
                 vector_step(s)
             for job in fixes:
                 fix_job(job)
             if s % NB == NB - 1:
-                if pending is not None and REST_ENG[pending] == "v":
+                if pending is not None:
                     chunk_rest(pending, "v")
                 while x_done < x_copied:
                     count = 2 if (x_copied - x_done >= 2 and x_done % 2 == 0) else 1
                     quantize_x(x_done, count)
                     x_done += count
                 while to_cast:
-                    job, was = to_cast.pop(0)
-                    cast_job(job, CAST_ENG)
+                    cast_job(to_cast.pop(0), CAST_ENG)
                 while to_quant:
                     quantize_pair()
                 if pending is not None:
                     chunk_quantize(pending, s)
                     pending = None
         last = len(UNITS) - 1
-        it = n_steps
-        interleave("a", il_tail[:, 0:TAIL_ACT_COLS, :], last, 0, TAIL_ACT_COLS)
-        interleave("v", il_tail[:, TAIL_ACT_COLS:BLK, :], last, TAIL_ACT_COLS, BLK - TAIL_ACT_COLS)
+        it = n_steps - 1
+        w0, w1, w2, w3, n0, n1, n23, n45 = JOBS[9:]
         r_passes(it)
+        interleave("a", il_tail[:, 0:BLK, :], last, 0, BLK)
+        vector_step(it)
+        r_passes(it + 1)
+        chunk_quantize(pending, it + 1)
         interleave("a", il_tail[:, BLK:BLK + TAIL_P_COLS, :], last, BLK, TAIL_P_COLS)
         interleave("v", il_tail[:, BLK + TAIL_P_COLS:512, :], last, BLK + TAIL_P_COLS, BLK - TAIL_P_COLS)
         quantize_pz(last, 0, BLK, il_tail[:, 0:BLK, :], it)
         quantize_pz(last, BLK, BLK, il_tail[:, BLK:512, :], it)
-        wide = JOBS[12:16]
-        narrow = JOBS[16:20]
-        late = [(4, 768, 256, narrow[0][3], it, "a"), (5, 768, 256, narrow[1][3], it, "v")]
-        for job in narrow + wide:
-            r_pass(job, 3)
+        quantize_pair()
+        for job in (n0, n1, w0, w1, n0, n1, w0, w1, w2, w3, w2, w3):
+            r_pass(job)
 
-        def finish(a, b):
-            for job in (a, b):
-                empty_job(job, it)
-                fix_job(job)
+        def finish(job, eng):
+            empty_job(job, eng)
+            fix_job(job)
 
-        def casts(a, b):
-            for job in (a, b):
-                cast_job(job, TAIL_CAST[len(stored)])
-
-        finish(*narrow[0:2])
-        for job in late:
-            for grp in range(4):
-                r_pass(job, grp)
-        finish(*narrow[2:4])
-        casts(*narrow[0:2])
-        finish(*wide[0:2])
-        casts(*narrow[2:4])
-        turn_pair(0, 1, narrow[2][3], it)
-        turn_pair(1, 1, narrow[3][3], it)
-        finish(*wide[2:4])
-        casts(*wide[0:2])
+        finish(n0, "a")
+        finish(n1, "v")
+        cast_job(n0, "v")
+        cast_job(n1, "v")
+        finish(w0, "a")
+        finish(w1, "v")
+        for n in range(6):
+            r_pass(n23)
+        turn_pair(0, 1, n0[3], it)
+        for n in range(6):
+            r_pass(n45)
+        finish(w2, "a")
+        cast_job(w0, "v")
+        cast_job(w1, "v")
+        finish(w3, "a")
+        turn_pair(3, 0, n1[3], it)
+        finish(n23, "v")
         copy_pair(it, "a")
-        turn_pair(3, 0, wide[0][3], it)
-        finish(*late)
-        casts(*wide[2:4])
+        cast_job(w2, "v")
+        cast_job(w3, "v")
+        finish(n45, "a")
+        turn_pair(3, 1, w0[3], it)
+        cast_job(n23, "v")
         quantize_pair()
         copy_pair(it, "a")
-        turn_pair(3, 1, wide[1][3], it)
-        casts(*late)
-        turn_pair(2, 1, wide[2][3], it)
-        copy_pair(it, "a")
-        quantize_pair()
-        quantize_pair()
+        cast_job(n45, "v")
+        turn_pair(1, 1, w1[3], it)
+        turn_pair(2, 1, w2[3], it)
         copy_pair(it, "v")
+        quantize_pair()
+        copy_pair(it, "a")
+        quantize_pair()
         copy_pair(it, "a")
         quantize_pair()
         quantize_pair()

import math
from contextlib import ExitStack

import concourse.mybir as mybir
from concourse.masks import make_identity

N, D = 2048, 1024
FLOPS = 2 * N * D * D * 2

F32 = mybir.dt.float32
BF16 = mybir.dt.bfloat16
U32 = mybir.dt.uint32
I32 = mybir.dt.int32
U8 = mybir.dt.uint8
FP8X4 = mybir.dt.float8_e4m3fn_x4
ALU = mybir.AluOpType
ACT = mybir.ActivationFunctionType

P = 128
BLK = 256
ROOT_N = math.sqrt(N)

UNITS = [(0, 0), (1, 0), (2, 0), (0, 1), (1, 1), (0, 2), (1, 2), (0, 3), (1, 3),
         (2, 1), (2, 2), (2, 3), (3, 0), (3, 1), (3, 2), (3, 3)]
STEPS = [(0, 0), (1, 0), (0, 1), (1, 1)] + [(u, e) for u in range(2, 16) for e in range(2)]
POOL_SHARE = [272] + [352] * 14
NB = 2
POOL_COLS = 352
NY = 3
X_TURN = {1: [5, 6], 2: [7], 3: [8], 4: [9], 5: [10], 6: [11], 7: [12], 8: [13], 9: [14], 10: [15]}
X_COPY = "avaaaaaaaaaaaaaa"
X_BANK = [4, 5, 6, 7, 4, 5, 6, 7, 4, 5, 4, 5, 4, 5, 4, 5]
JOBS = [((0,), 0, 512, 6, 8, "a"), ((1,), 0, 512, 7, 8, "a"), ((2,), 0, 512, 4, 13, "a"), ((3,), 0, 512, 5, 14, "a"),
        ((4,), 0, 512, 6, 22, "a"), ((5,), 0, 512, 7, 23, "a"), ((0, 1), 512, 256, 4, 25, "a"), ((2, 3), 512, 256, 5, 27, "a"),
        ((4, 5), 512, 256, 6, 28, "a"), ((6,), 0, 512, 7, 28, "a"), ((7,), 0, 512, 5, 29, "v"), ((6,), 512, 512, 6, 30, "a"),
        ((7,), 512, 512, 4, 31, "v"), ((0,), 768, 256, 3, 30, "a"), ((1,), 768, 256, 1, 31, "v"), ((2, 3), 768, 256, 0, 32, "a"),
        ((4, 5), 768, 256, 2, 32, "v")]
TURNS = {23: (0, 0, 4), 24: (1, 0, 5), 29: (2, 0, 4)}
EMPTY_MAX = 2
ACT_SHARE = [0, 0, 0, 0, 0, 160, 160, 160, 160, 160, 160, 160, 0, 0, 160]
FAST_IL = True
CAST_ENG = "v"
TAIL_P_COLS = 96


def p_at(col):
    b = col // BLK
    return 512 * b + (BLK if b % 2 else 0) + col % BLK


def z_at(col):
    b = col // BLK
    return 512 * b + (0 if b % 2 else BLK) + col % BLK


def tile_extendedinfomaxnaturalgradient_x2_kernel(tc, x, w_words, w_scales, k, g, h, out_0, out_1, out_2):
    nc = tc.nc
    with ExitStack() as ctx:
        sb = ctx.enter_context(tc.tile_pool(name="sb", bufs=1))
        ps = ctx.enter_context(tc.psum_pool(name="ps", bufs=1))
        ctx.enter_context(tc.manual_schedule())

        banks = [ps.tile([P, 512], F32, name="bank%d" % b) for b in range(8)]
        x_raw = [sb.tile([P, D], BF16, name="x_raw%d" % m, align_bytes=64) for m in range(16)]
        x_il = sb.tile([P, 8, D], BF16, name="x_il", align_bytes=64)
        x_codes = sb.tile([P, 16 * 256], U32, name="x_codes", align_bytes=64)
        x_scales = sb.tile([P, 16 * 256], U8, name="x_scales", align_bytes=64)
        w_codes = [sb.tile([P, 2, BLK], U32, name="w_codes%d" % a, align_bytes=64) for a in range(4)]
        w_plane = sb.tile([P, D], U8, name="w_plane", align_bytes=64)
        k_cols = sb.tile([P, 2, 4], BF16, name="k_cols")
        g_raw = sb.tile([P, 4, 4], BF16, name="g_raw")
        h_raw = sb.tile([P, 4, 4], BF16, name="h_raw")
        g_col = sb.tile([P, 4, 4], F32, name="g_col")
        h_col = sb.tile([P, 4, 4], F32, name="h_col")
        ident = sb.tile([P, P], F32, name="ident")
        ident_bf = sb.tile([P, P], BF16, name="ident_bf")
        ident_root = sb.tile([P, P], F32, name="ident_root")
        warm = sb.tile([P, 2], F32, name="warm")
        tanh_y = [sb.tile([P, 512], F32, name="tanh_y%d" % a) for a in range(3)]
        gk_tanh = [sb.tile([P, BLK], F32, name="gk_tanh%d" % a) for a in range(2)]
        stage = [sb.tile([P, 4, 512], BF16, name="stage%d" % a, align_bytes=64) for a in range(3)]
        chunk_cols = BLK * NB
        pool_cols = POOL_COLS * NB // 2
        rest_cols = chunk_cols - pool_cols
        il = sb.tile([P, 2 * rest_cols + pool_cols, 4], BF16, name="il", align_bytes=64)
        il_tail = sb.tile([P, 512, 4], BF16, name="il_tail", align_bytes=64)
        pz_codes = sb.tile([P, 4, 2048], U32, name="pz_codes", align_bytes=64)
        pz_scales = sb.tile([P, 4, 2048], U8, name="pz_scales", align_bytes=64)
        r32 = sb.tile([P, 8, D], F32, name="r32")
        r16 = sb.tile([P, 8, 2, 2, P, 2], BF16, name="r16", align_bytes=64)
        r_il = [sb.tile([P, 2, P, 4], BF16, name="r_il%d" % a, align_bytes=64) for a in range(4)]
        o_codes = sb.tile([P, 2, D], U32, name="o_codes", align_bytes=64)
        o_scales = sb.tile([P, 2, D], U8, name="o_scales", align_bytes=64)

        k_bank = banks[0][:].bitcast(BF16)
        y_banks = banks[1:1 + NY]

        x_rows = x.rearrange("(a p t) j -> a t p j", p=P, t=4)
        w_view = w_words.rearrange("a p n t -> p a (n t)")

        def load_x(m):
            nc.sync.dma_start(out=x_raw[m][:], in_=x_rows[m // 4, m % 4])

        def load_w(half):
            nc.sync.dma_start(out=w_codes[half][:].bitcast(I32), in_=w_view[:, :, 1024 * half:1024 * (half + 1)].bitcast(I32))

        make_identity(nc, ident[:])
        nc.vector.memset(w_plane[:].bitcast(I32), 0)
        nc.vector.memset(warm[:], 0.0)
        nc.scalar.dma_start(out=k_cols[:], in_=k.rearrange("(a p c) -> p a c", a=2, c=4))
        load_x(0)
        load_x(1)
        load_w(0)
        for q in range(4):
            nc.scalar.dma_start(out=w_plane[32 * q:32 * q + 8, :].bitcast(I32), in_=w_scales[:, 4 * q:4 * q + 4, :].bitcast(I32))
        nc.scalar.activation(out=warm[:, 1:2], in_=warm[:, 0:1], func=ACT.Tanh)
        nc.gpsimd.dma_start(out=h_raw[:], in_=h.rearrange("(a p t) -> p a t", a=4, t=4))
        nc.gpsimd.dma_start(out=g_raw[:], in_=g.rearrange("(a p t) -> p a t", a=4, t=4))
        for m in range(2, 16):
            load_x(m)
            if m == 2:
                load_w(1)
            if m == 5:
                load_w(2)
        load_w(3)
        nc.vector.tensor_copy(out=ident_bf[:], in_=ident[:])
        nc.vector.tensor_scalar(out=ident_root[:], in0=ident[:], scalar1=ROOT_N, scalar2=None, op0=ALU.mult)

        def turn_x(m):
            words = x_raw[m][:].bitcast(F32)
            bank = banks[X_BANK[m]]
            for a in range(2):
                for u in range(2):
                    c = (2 * a + u) * P
                    nc.tensor.transpose(bank[:, c:c + P], words[:, 256 * a + u:256 * (a + 1):2], ident[:])

        def copy_x(m, eng):
            src = banks[X_BANK[m]][:].rearrange("p (a u r) -> p a r u", a=2, u=2)
            dst = x_il[:, m % 8, :].bitcast(F32).rearrange("p (a r u) -> p a r u", a=2, u=2)
            if eng == "a":
                nc.scalar.copy(out=dst, in_=src)
            else:
                nc.vector.tensor_copy(out=dst, in_=src)

        def quantize_x(m, count):
            cols = slice(256 * m, 256 * (m + count))
            nc.vector.quantize_mx(out=x_codes[:, cols].bitcast(FP8X4), scales=x_scales[:, cols],
                                  in_=x_il[:, m % 8:m % 8 + count, :].rearrange("p a c -> p (a c)"))

        def spread_k(a):
            for c in range(4):
                    o = (4 * a + c) * P
                    nc.tensor.transpose(k_bank[:, o:o + P], k_cols[:, a, c:c + 1].to_broadcast([P, P]), ident_bf[:])

        def y_step(s, tiles=(0, 1)):
            unit, half = STEPS[s]
            b, grp = UNITS[unit]
            bank = y_banks[s % NY]
            for e in tiles:
                m = 4 * grp + 2 * half + e
                for a in range(2):
                    xc = slice(256 * m + P * a, 256 * m + P * (a + 1))
                    nc.tensor.matmul_mx(out=bank[:, BLK * e:BLK * (e + 1)], lhsT=x_codes[:, xc].bitcast(FP8X4), lhsT_scale=x_scales[:, xc],
                                        rhs=w_codes[b][:, a, :].bitcast(FP8X4), rhs_scale=w_plane[4 * a:, BLK * b:BLK * (b + 1)],
                                        start=(a == 0), stop=(a == 1))

        def scalar_step(s):
            unit, half = STEPS[s]
            b, grp = UNITS[unit]
            bank = y_banks[s % NY]
            nc.scalar.activation(out=tanh_y[s % 3][:], in_=bank[:], func=ACT.Tanh)
            zc = z_at(BLK * b) - 512 * b
            for e in range(2):
                t = 2 * half + e
                nc.scalar.activation(out=stage[unit % 3][:, t, zc:zc + BLK], in_=bank[:, BLK * e:BLK * (e + 1)],
                                     func=ACT.Copy, scale=h_col[:, grp, t:t + 1])

        def vector_step(s):
            unit, half = STEPS[s]
            b, grp = UNITS[unit]
            bank = y_banks[s % NY]
            pc = p_at(BLK * b) - 512 * b
            k_row = k_bank[:, 512 * (b // 2):512 * (b // 2 + 1)].rearrange("p (c r) -> p r c", c=4)[:, 64 * (b % 2):64 * (b % 2 + 1), :]
            for e in range(2):
                t = 2 * half + e
                nc.vector.scalar_tensor_tensor(out=gk_tanh[e][:].rearrange("p (r c) -> p r c", c=4),
                                               in0=tanh_y[s % 3][:, BLK * e:BLK * (e + 1)].rearrange("p (r c) -> p r c", c=4),
                                               scalar=g_col[:, grp, t:t + 1], in1=k_row, op0=ALU.mult, op1=ALU.mult)
            for e in range(2):
                t = 2 * half + e
                nc.vector.scalar_tensor_tensor(out=stage[unit % 3][:, t, pc:pc + BLK], in0=bank[:, BLK * e:BLK * (e + 1)],
                                               scalar=g_col[:, grp, t:t + 1], in1=gk_tanh[e][:], op0=ALU.mult, op1=ALU.add)

        def interleave(eng, dst, unit, c0, cols):
            src = stage[unit % 3][:, :, c0:c0 + cols].rearrange("p t c -> p c t")
            if eng == "p":
                nc.gpsimd.tensor_scalar(out=dst, in0=src, scalar1=1.0, scalar2=1.0, op0=ALU.mult, op1=ALU.mult)
                return
            if FAST_IL:
                dst = dst.rearrange("p (c i) t -> p c t i", i=4)
                src = src.rearrange("p (c i) t -> p c t i", i=4)
            if eng == "a":
                nc.scalar.copy(out=dst, in_=src)
            else:
                nc.vector.tensor_copy(out=dst, in_=src)

        def chunk_base(c):
            return 0 if c % 2 == 0 else rest_cols

        def chunk_pool(c):
            n = POOL_SHARE[c]
            c0 = 512 - n if c % 2 == 0 else 0
            interleave("p", il[:, chunk_base(c) + c0:chunk_base(c) + c0 + n, :], c, c0, n)

        def chunk_rest(c, eng):
            n = ACT_SHARE[c] if eng == "a" else 512 - POOL_SHARE[c] - ACT_SHARE[c]
            edge = 0 if eng == "a" else ACT_SHARE[c]
            c0 = edge if c % 2 == 0 else 512 - edge - n
            if n:
                interleave(eng, il[:, chunk_base(c) + c0:chunk_base(c) + c0 + n, :], c, c0, n)

        made = {}

        def quantize_pz(unit, c0, cols, src, it):
            b, grp = UNITS[unit]
            at = slice(512 * b + c0, 512 * b + c0 + cols)
            nc.vector.quantize_mx(out=pz_codes[:, grp, at].bitcast(FP8X4), scales=pz_scales[:, grp, at], in_=src.rearrange("p c t -> p (c t)"))
            for c in range(512 * b + c0, 512 * b + c0 + cols, BLK):
                made[(grp, c // BLK)] = it

        def chunk_quantize(c, it):
            quantize_pz(c, 0, 512, il[:, chunk_base(c):chunk_base(c) + 512, :], it)

        passes_done = {}
        to_empty = []
        to_cast = []
        to_copy = []
        to_quant = []
        stored = []

        def ready(job, n, it):
            tiles, j0, w = job[:3]
            need = [p_at(P * tiles[n // 4]) // BLK] + [z_at(c) // BLK for c in range(j0, j0 + w, BLK)]
            return all((n % 4, c) in made and made[(n % 4, c)] < it for c in need)

        def r_pass(job):
            tiles, j0, w, b = job[:4]
            n = passes_done.get(job, 0)
            passes_done[job] = n + 1
            e, grp = divmod(n, 4)
            pc = slice(p_at(P * tiles[e]), p_at(P * tiles[e]) + P)
            zc = slice(z_at(j0), z_at(j0) + w)
            nc.tensor.matmul_mx(out=banks[b][:, w * e:w * (e + 1)], lhsT=pz_codes[:, grp, pc].bitcast(FP8X4), lhsT_scale=pz_scales[:, grp, pc],
                                rhs=pz_codes[:, grp, zc].bitcast(FP8X4), rhs_scale=pz_scales[:, grp, zc], start=(grp == 0), stop=(grp == 3))

        def r_passes(it):
            for job in JOBS:
                total = 4 * len(job[0])
                while job[4] <= it and passes_done.get(job, 0) < total and ready(job, passes_done.get(job, 0), it):
                    r_pass(job)
                    if passes_done[job] == total:
                        to_empty.append((job, it))

        def empty_job(job, eng):
            tiles, j0, w, b = job[:4]
            dst = r32[:, tiles[0]:tiles[-1] + 1, j0:j0 + w]
            src = banks[b][:, 0:w * len(tiles)].rearrange("p (e c) -> p e c", c=w)
            if eng == "a":
                nc.scalar.activation(out=dst, in_=src, func=ACT.Copy, scale=-1.0 / ROOT_N)
            else:
                nc.vector.tensor_scalar(out=dst, in0=src, scalar1=-1.0 / ROOT_N, scalar2=None, op0=ALU.mult)

        def fix_job(job):
            tiles, j0, w, b = job[:4]
            for e, i in enumerate(tiles):
                d = P * i - j0
                if 0 <= d < w:
                    nc.vector.scalar_tensor_tensor(out=r32[:, i, P * i:P * (i + 1)], in0=banks[b][:, w * e + d:w * e + d + P], scalar=-1.0 / ROOT_N,
                                                   in1=ident_root[:], op0=ALU.mult, op1=ALU.add)
            rows = out_0[P * tiles[0]:P * (tiles[-1] + 1), j0:j0 + w].rearrange("(e p) c -> p e c", p=P)
            nc.sync.dma_start(out=rows, in_=r32[:, tiles[0]:tiles[-1] + 1, j0:j0 + w])

        def cast_job(job, eng):
            tiles, j0, w = job[:3]
            a, r0 = j0 // 512, (j0 % 512) // 4
            for i in tiles:
                dst = r16[:, i, a, :, r0:r0 + w // 4, :]
                src = r32[:, i, j0:j0 + w].rearrange("p (r u e) -> p u r e", u=2, e=2)
                if eng == "p":
                    nc.gpsimd.tensor_scalar(out=dst, in0=src, scalar1=1.0, scalar2=1.0, op0=ALU.mult, op1=ALU.mult)
                elif eng == "a":
                    nc.scalar.copy(out=dst, in_=src)
                else:
                    nc.vector.tensor_copy(out=dst, in_=src)

        def turn_pair(pair, a, b, it):
            for e in range(2):
                for u in range(2):
                    c = (2 * e + u) * P
                    nc.tensor.transpose(banks[b][:, c:c + P], r16[:, 2 * pair + e, a, u].rearrange("p r e -> p (r e)").bitcast(F32), ident[:])
            to_copy.append((pair, a, b, it))

        def copy_pair(it, eng):
            pair, a, b, was = to_copy.pop(0)
            slot = len(stored) % 4
            stored.append(pair)
            src = banks[b][:].rearrange("p (e u r) -> p e r u", e=2, u=2)
            dst = r_il[slot][:].rearrange("p e r t -> p (e r t)").bitcast(F32).rearrange("p (e r u) -> p e r u", e=2, u=2)
            if eng == "a":
                nc.scalar.copy(out=dst, in_=src)
            else:
                nc.vector.tensor_copy(out=dst, in_=src)
            to_quant.append((pair, a, slot, it))

        def quantize_pair():
            pair, a, slot, was = to_quant.pop(0)
            at = slice(BLK * pair, BLK * (pair + 1))
            nc.vector.quantize_mx(out=o_codes[:, a, at].bitcast(FP8X4), scales=o_scales[:, a, at], in_=r_il[slot][:].rearrange("p e r t -> p (e r t)"))
            nc.sync.dma_start(out=out_1[a].rearrange("p m t -> p (m t)")[:, 4 * BLK * pair:4 * BLK * (pair + 1)].bitcast(I32), in_=o_codes[:, a, at].bitcast(I32))

        n_steps = len(STEPS)
        spread_k(0)
        turn_x(0)
        turn_x(1)
        copy_x(0, X_COPY[0])
        quantize_x(0, 1)
        copy_x(1, X_COPY[1])
        nc.vector.tensor_copy(out=h_col[:], in_=h_raw[:])
        quantize_x(1, 1)
        nc.vector.tensor_copy(out=g_col[:], in_=g_raw[:])
        turn_x(2)
        y_step(0)
        turn_x(3)
        y_step(1)
        copy_x(2, X_COPY[2])
        scalar_step(0)
        quantize_x(2, 1)
        vector_step(0)
        copy_x(3, X_COPY[3])
        quantize_x(3, 1)
        y_step(2)
        turn_x(4)
        scalar_step(1)
        spread_k(1)
        x_done = 4
        x_copied = 4
        x_turned = 5
        chunk = 0
        pending = None
        for s in range(1, n_steps - 1):
            x_to_copy = x_turned
            if s + 2 < n_steps:
                y_step(s + 2)
            for m in X_TURN.get(s, []):
                turn_x(m)
                x_turned += 1
            if s in TURNS:
                turn_pair(*TURNS[s], s)
            r_passes(s)
            fresh = pending is None and (chunk, 1) in STEPS[:max(s, 0)] and chunk <= s // 2 - 1
            if fresh:
                pending = chunk
                chunk += 1
                chunk_pool(pending)
            while x_copied < x_to_copy:
                copy_x(x_copied, X_COPY[x_copied])
                x_copied += 1
            if to_copy and to_copy[0][3] < s:
                copy_pair(s, "a")
            fixes = []
            while to_empty and to_empty[0][1] < s and len(fixes) < EMPTY_MAX:
                job, was = to_empty.pop(0)
                empty_job(job, job[5])
                to_cast.append(job)
                fixes.append(job)
            if 0 < s + 1 < n_steps:
                scalar_step(s + 1)
            if fresh:
                chunk_rest(pending, "a")
            if s >= 0:
                vector_step(s)
            for job in fixes:
                fix_job(job)
            if s % NB == NB - 1:
                if pending is not None:
                    chunk_rest(pending, "v")
                while x_done < x_copied:
                    count = 2 if (x_copied - x_done >= 2 and x_done % 2 == 0) else 1
                    quantize_x(x_done, count)
                    x_done += count
                while to_cast:
                    cast_job(to_cast.pop(0), CAST_ENG)
                while to_quant:
                    quantize_pair()
                if pending is not None:
                    chunk_quantize(pending, s)
                    pending = None
        last = len(UNITS) - 1
        it = n_steps - 1
        w0, w1, w2, w3, n0, n1, n23, n45 = JOBS[9:]
        r_passes(it)
        interleave("a", il_tail[:, 0:BLK, :], last, 0, BLK)
        vector_step(it)
        r_passes(it + 1)
        chunk_quantize(pending, it + 1)
        interleave("a", il_tail[:, BLK:BLK + TAIL_P_COLS, :], last, BLK, TAIL_P_COLS)
        interleave("v", il_tail[:, BLK + TAIL_P_COLS:512, :], last, BLK + TAIL_P_COLS, BLK - TAIL_P_COLS)
        quantize_pz(last, 0, BLK, il_tail[:, 0:BLK, :], it)
        quantize_pz(last, BLK, BLK, il_tail[:, BLK:512, :], it)
        quantize_pair()
        for job in (n0, n1, w0, w1, n0, n1, w0, w1, w2, w3, w2, w3):
            r_pass(job)

        def finish(job, eng):
            empty_job(job, eng)
            fix_job(job)

        finish(n0, "a")
        finish(n1, "v")
        cast_job(n0, "v")
        cast_job(n1, "v")
        finish(w0, "a")
        finish(w1, "v")
        for n in range(6):
            r_pass(n23)
        turn_pair(0, 1, n0[3], it)
        for n in range(6):
            r_pass(n45)
        finish(w2, "a")
        cast_job(w0, "v")
        cast_job(w1, "v")
        finish(w3, "a")
        turn_pair(3, 0, n1[3], it)
        finish(n23, "v")
        copy_pair(it, "a")
        cast_job(w2, "v")
        cast_job(w3, "v")
        finish(n45, "a")
        turn_pair(3, 1, w0[3], it)
        cast_job(n23, "v")
        quantize_pair()
        copy_pair(it, "a")
        cast_job(n45, "v")
        turn_pair(1, 1, w1[3], it)
        turn_pair(2, 1, w2[3], it)
        copy_pair(it, "v")
        quantize_pair()
        copy_pair(it, "a")
        quantize_pair()
        copy_pair(it, "a")
        quantize_pair()
        quantize_pair()
        for q in range(4):
            eng = nc.sync if q % 2 else nc.scalar
            eng.dma_start(out=out_2[:, 4 * q:4 * q + 4, :].rearrange("a r m -> r a m").bitcast(I32), in_=o_scales[32 * q:32 * q + 4, :, :].bitcast(I32))
